import numpy as np
import ml_dtypes


def mxq(x, axis, fmt="e4m3"):
    dtype, down = {"e4m3": (ml_dtypes.float8_e4m3fn, 7), "e5m2": (ml_dtypes.float8_e5m2, 14)}[fmt]
    v = np.moveaxis(np.asarray(x, np.float32).astype(ml_dtypes.bfloat16).astype(np.float64), axis, -1)
    blocks = v.reshape(v.shape[:-1] + (-1, 32))
    amax = np.abs(blocks).max(-1, keepdims=True)
    byte = np.maximum(np.where(amax > 0, np.frexp(amax)[1] - 1 + 127, 0) - down, 1)
    scale = np.exp2(byte - 127.0)
    codes = (blocks / scale).astype(np.float32).astype(dtype).astype(np.float64)
    return np.moveaxis((codes * scale).reshape(v.shape), -1, axis)


WIDE = False


def mx_kscale(k):
    if not WIDE:
        return np.ones(k)
    levels = np.array([10, -10, 5, -5, 0])
    if k % 512:
        return np.exp2(np.random.permutation(np.resize(levels, k // 32))).repeat(32)
    a = np.empty((k // 512, 16))
    for p in range(k // 512):
        a[p, :8] = np.random.permutation(np.resize(levels, 8))
        for g in range(8):
            far = levels[np.abs(levels - a[p, g]) >= 10]
            a[p, g + 8] = far[np.random.randint(len(far))]
    return np.exp2(a.ravel()).repeat(32)


def f64(x):
    return np.asarray(x).astype(np.float64)


def striped(idx):
    return np.tile(idx.reshape(-1, 16).T, (8, 1)).astype(np.uint16)


def unstriped(offs):
    return offs[:16].T.reshape(-1).astype(np.int64)


E2M1 = np.array([0.0, 0.5, 1.0, 1.5, 2.0, 3.0, 4.0, 6.0, -0.0, -0.5, -1.0, -1.5, -2.0, -3.0, -4.0, -6.0])


def pack_weight(w, fmt):
    k, n = w.shape
    w = f64(np.asarray(w, np.float32).astype(ml_dtypes.bfloat16)).reshape(k // 32, 32, n)
    amax = np.abs(w).max(1)
    if fmt == "e4m3":
        byte = np.frexp(amax)[1] - 1 + 127 - 7
    else:
        mant, ex = np.frexp(amax / 6.0)
        byte = np.where(mant > 0.5, ex, ex - 1) + 127
    byte = np.clip(np.where(amax > 0, byte, 1), 1, 254)
    scaled = (w * np.exp2(127.0 - byte)[:, None, :]).reshape(k, n).astype(np.float32)
    by_word = np.ascontiguousarray(scaled.reshape(k // 512, 128, 4, n).transpose(0, 1, 3, 2))
    if fmt == "e4m3":
        words = by_word.astype(ml_dtypes.float8_e4m3fn).view(np.uint8)
    else:
        c = by_word.astype(ml_dtypes.float4_e2m1fn).view(np.uint8) & 0xF
        words = (c[..., 0::2] | (c[..., 1::2] << 4)).reshape(k // 512, 128, 2 * n)
    return np.ascontiguousarray(words), np.ascontiguousarray(byte.astype(np.uint8).reshape(k // 512, 16, n))


def unpack_weight(words, scales, fmt):
    g, _, n = scales.shape
    words = np.ascontiguousarray(words).reshape(g, 128, n, -1)
    if fmt == "e4m3":
        vals = words.view(ml_dtypes.float8_e4m3fn).astype(np.float64)
    else:
        nib = np.empty((g, 128, n, 4), np.uint8)
        nib[..., 0::2] = words & 0xF
        nib[..., 1::2] = words >> 4
        vals = E2M1[nib]
    vals = vals * np.repeat(np.exp2(scales.astype(np.float64) - 127.0), 8, axis=1)[..., None]
    return vals.transpose(0, 1, 3, 2).reshape(g * 512, n)


def gelu(v):
    return 0.5 * v * (1.0 + np.tanh(np.sqrt(2.0 / np.pi) * (v + 0.044715 * v**3)))


def striped8(idx):
    return np.concatenate([v.reshape(-1, 16).T for v in idx]).astype(np.uint16)


def unstriped8(offs):
    return np.stack([offs[16 * g:16 * g + 16].T.reshape(-1) for g in range(8)]).astype(np.int64)


def heads(h, wgt, idx8):
    r = np.arange(h.shape[0])
    return wgt[r // 4 % 128] * h[r[:, None], idx8[r % 512 // 64]]


def put_heads(h, wgs, idx8, t2):
    r = np.arange(h.shape[0])
    page = np.zeros((h.shape[0], t2))
    page[r[:, None], idx8[r % 512 // 64]] = wgs[r // 4 % 128] * h
    return page


K, T, S, H, T2, P, N = 1024, 2048, 1024, 1024, 2048, 1024, 512

def setup_inputs():
    n = np.random.standard_normal
    s = mx_kscale(K)[:, None]
    u = mx_kscale(H)[:, None]
    d = {}
    d["tab_words"], d["tab_scales"] = pack_weight(n((K, T)) * s, "e4m3")
    d["offs"] = striped(np.random.permutation(T)[:S])
    d["w1"] = (0.33 * n((K, H)) / K**0.5 / s).astype(np.float32)
    d["phase"] = np.random.uniform(-1.2, 1.2, H).astype(np.float32)
    d["gain"] = (np.exp(0.3 * n(H)) * u[:, 0]).astype(np.float32)
    d["wgs"] = np.repeat(np.random.uniform(0.5, 2.0, (8, S)), 16, axis=0).astype(np.float32)
    d["offs2"] = striped8(np.stack([np.random.permutation(T2)[:S] for _ in range(8)]))
    d["wgt"] = np.repeat(np.random.uniform(0.5, 2.0, (8, P)), 16, axis=0).astype(np.float32)
    d["offs3"] = striped8(np.stack([np.random.permutation(T2)[:P] for _ in range(8)]))
    d["press"] = (0.8 * n((H, P)) * u).astype(np.float32)
    d["w2"] = (n((H, N)) / H**0.5 / u).astype(np.float32)
    d["w4_words"], d["w4_scales"] = pack_weight(n((H, N)) / H**0.5 / u, "e2m1")
    d["b"] = (0.5 * n(N)).astype(np.float32)
    return d

def reference(tab_words, tab_scales, offs, w1, phase, gain, wgs, offs2, wgt, offs3, press, w2, w4_words, w4_scales, b):
    v = unpack_weight(tab_words, tab_scales, "e4m3")[:, unstriped(offs)]
    w4 = unpack_weight(w4_words, w4_scales, "e2m1")
    f = mxq(f64(w1), 0, "e4m3").T @ v
    h = f64(gain)[:, None] * (f + np.sin(f + f64(phase)[:, None]))
    page = put_heads(h, f64(wgs), unstriped8(offs2), T2)
    x = heads(page, f64(wgt), unstriped8(offs3))
    z = x + f64(press)
    zq = mxq(z, 0, "e4m3")
    y1 = mxq(f64(w2), 0, "e4m3").T @ zq
    y2 = w4.T @ zq
    return np.maximum(y1 + f64(b)[:, None], y2)

@@ -1,0 +1,384 @@
+import math
+from contextlib import ExitStack
+
+import concourse.mybir as mybir
+from concourse.masks import make_identity
+
+K, T, S, H, T2, M, N = 1024, 2048, 1024, 1024, 2048, 1024, 512
+FLOPS = 2 * K * H * S + 2 * 2 * H * N * M
+
+F32 = mybir.dt.float32
+BF16 = mybir.dt.bfloat16
+I32 = mybir.dt.int32
+U32 = mybir.dt.uint32
+U16 = mybir.dt.uint16
+U8 = mybir.dt.uint8
+FP8X4 = mybir.dt.float8_e4m3fn_x4
+FP4X4 = mybir.dt.float4_e2m1fn_x4
+ACT = mybir.ActivationFunctionType
+ALU = mybir.AluOpType
+
+P = 128
+PACK = 4
+PASS = P * PACK
+BANK = 512
+SLICES = H // P
+FIRST_PIECES = ((0, 256), (256, 512), (512, 1024))
+UNITS = [(0, j0, j1) for j0, j1 in FIRST_PIECES] + [(s, j0, j0 + BANK) for s in range(1, SLICES) for j0 in (0, BANK)]
+CHUNK = 256
+CHUNKS = ((0, 256), (256, 512), (512, 768), (768, 896), (896, 1024))
+CAST_AFTER_UNIT = (4, 6, 10, 12)
+TWO_PI = 2.0 * math.pi
+TURNS_MID = 98304.0
+TURNS_MID_BITS = float(0x47C00000)
+BITS_PER_TURN = 128.0
+
+
+def tile_list_fountain_cue_scorer_kernel(
+    tc, tab_words, tab_scales, offs, w1, phase, gain, wgs, offs2, wgt, offs3, press, w2, w4_words, w4_scales, b, out
+):
+    nc = tc.nc
+    with ExitStack() as ctx:
+        keep = ctx.enter_context(tc.tile_pool(name="keep", bufs=1))
+        ring = ctx.enter_context(tc.tile_pool(name="ring", bufs=3))
+        psum = ctx.enter_context(tc.psum_pool(name="psum", bufs=1))
+
+        def held(name, shape, dtype):
+            return keep.tile(shape, dtype, name=name, align_bytes=64)
+
+        def pair_of(name, shape, dtype, count=2):
+            return [held("%s%d" % (name, n), shape, dtype) for n in range(count)]
+
+        bank = {}
+        for role in ("f", "full", "frac", "both"):
+            for n in range(2):
+                bank[role, n] = psum.tile([P, BANK], F32, name="bank_%s%d" % (role, n))
+
+        tab_sc = held("tab_sc", [P, T], U8)
+        nc.gpsimd.memset(tab_sc[:].bitcast(I32), 0)
+        minus_mid = held("minus_mid", [P, P], F32)
+        nc.vector.memset(minus_mid[:], -TURNS_MID)
+        ident = held("ident", [P, P], F32)
+        make_identity(nc, ident[:])
+        pages = pair_of("page", [P, T2], F32, PACK)
+        for page in pages:
+            nc.vector.memset(page[:], 0.0)
+
+        for q in range(4):
+            nc.scalar.dma_start(
+                out=tab_sc[32 * q : 32 * q + 8, :].bitcast(I32), in_=tab_scales[:, 4 * q : 4 * q + 4, :].bitcast(I32)
+            )
+        warm = held("warm", [P, 1], F32)
+        nc.scalar.activation(warm[:], minus_mid[:, 0:1], ACT.Sin, scale=0.0)
+        pick = keep.tile([P, S // 16], U16, name="pick")
+        nc.sync.dma_start(pick[:], offs)
+        phase_sb = held("phase_sb", [P, 2, PACK], F32)
+        nc.sync.dma_start(out=phase_sb[:], in_=phase.rearrange("(b p i) -> p b i", b=2, i=PACK))
+        gain_sb = held("gain_sb", [P, 2, PACK], F32)
+        nc.sync.dma_start(out=gain_sb[:], in_=gain.rearrange("(b p i) -> p b i", b=2, i=PACK))
+        put = keep.tile([P, S // 16], U16, name="put")
+        nc.sync.dma_start(put[:], offs2)
+        take = keep.tile([P, M // 16], U16, name="take")
+        nc.sync.dma_start(take[:], offs3)
+        b_sb = held("b_sb", [P, N // P], F32)
+        with nc.allow_non_contiguous_dma(reason="one bias value for each output row"):
+            nc.gpsimd.dma_start(out=b_sb[:], in_=b.rearrange("(t p) -> p t", p=P))
+
+        weights = held("weights", [P, 2 * S], F32)
+        press_sb = held("press_sb", [P, PACK * M], F32)
+        stage = held("stage", [P, PACK * BANK], F32)
+        x_low = held("x_low", [P, PACK * M], F32)
+        x_late = x_low[:, 2 * M : 4 * M]
+
+        def load_rows(room, src, a, c0):
+            raw = room.rearrange("p (j c) -> p j c", j=PACK)
+            nc.sync.dma_start(
+                out=raw, in_=src[PASS * a : PASS * (a + 1), c0 : c0 + BANK].rearrange("(p j) c -> p j c", j=PACK)
+            )
+            return raw
+
+        w1_codes = {(a, blk): held("w1_codes%d%d" % (a, blk), [P, BANK], U32) for a in range(2) for blk in range(2)}
+        w1_scales = pair_of("w1_scales", [P, 2, BANK], U8)
+        w2_codes = pair_of("w2_codes", [P, N], U32)
+        w2_scales = pair_of("w2_scales", [P, N], U8)
+
+        def quantise_w1(raw, a, blk, copy, room):
+            grouped = room.bitcast(BF16)
+            copy(
+                out=grouped.rearrange("p (i m j) -> p m j i", i=PACK, j=PACK),
+                in_=raw.rearrange("p j (m i) -> p m j i", i=PACK),
+            )
+            nc.vector.quantize_mx(out=w1_codes[a, blk][:].bitcast(FP8X4), scales=w1_scales[blk][:, a, :], in_=grouped)
+
+        def quantise_w2(raw, blk, room):
+            grouped = room.bitcast(BF16)
+            nc.scalar.copy(
+                out=grouped.rearrange("p (c q j) -> p c j q", q=4, j=PACK),
+                in_=raw.rearrange("p j (c q) -> p c j q", q=4),
+            )
+            nc.vector.quantize_mx(out=w2_codes[blk][:].bitcast(FP8X4), scales=w2_scales[blk][:], in_=grouped)
+
+        w1_low = [load_rows(weights[:], w1, 0, 0), load_rows(press_sb[:, 0 : PACK * BANK], w1, 1, 0)]
+        tab_w = pair_of("tab_w", [P, T], I32)
+        for a in range(2):
+            nc.sync.dma_start(out=tab_w[a][:], in_=tab_words[a].rearrange("p t i -> p (t i)").bitcast(I32))
+
+        phase_turns = held("phase_turns", [P, 2, PACK], F32)
+        nc.vector.tensor_scalar(phase_turns[:], phase_sb[:], 1.0 / TWO_PI, None, ALU.mult)
+        h_bias = held("h_bias", [P, 2, PACK], F32)
+        nc.vector.scalar_tensor_tensor(h_bias[:], phase_sb[:], -1.0, gain_sb[:], ALU.mult, ALU.mult)
+
+        quantise_w1(w1_low[0], 0, 0, nc.vector.tensor_copy, stage[:, 0:S])
+        quantise_w1(w1_low[1], 1, 0, nc.scalar.copy, x_late[:, 0:S])
+        wgs_sb, wgt_sb = weights[:, 0:S], weights[:, S : S + M]
+        nc.sync.dma_start(out=wgs_sb, in_=wgs)
+        nc.sync.dma_start(out=wgt_sb, in_=wgt)
+        w1_high = [load_rows(stage[:], w1, 0, BANK), load_rows(x_late, w1, 1, BANK)]
+        press_rows = press_sb[:].rearrange("p (i m) -> p i m", i=PACK)
+
+        def load_press(blk):
+            nc.sync.dma_start(
+                out=press_rows, in_=press[PASS * blk : PASS * (blk + 1), :].rearrange("(p i) m -> p i m", i=PACK)
+            )
+
+        load_press(0)
+
+        v_sc = pair_of("v_sc", [P, BANK], U8)
+        v_w = {(a, half): held("v_w%d%d" % (a, half), [P, BANK], U32) for a in range(2) for half in range(2)}
+        for j0, j1 in FIRST_PIECES:
+            half, c0, c1 = j0 // BANK, j0 % BANK, (j1 - 1) % BANK + 1
+            cols = pick[:, j0 // 16 : j1 // 16]
+            nc.vector.tensor_copy(v_sc[half][:, c0:c1], tab_sc[:].indirect(cols))
+            for a in range(2):
+                nc.vector.tensor_copy(v_w[a, half][:, c0:c1], tab_w[a][:].bitcast(U32).indirect(cols))
+
+        turns_sb = pair_of("turns", [P, BANK], F32)
+        whole_sb = pair_of("whole", [P, BANK], U32)
+        terms_sb = pair_of("terms", [P, 2 * BANK], F32, 4)
+        h_ring = pair_of("h", [P, S], F32, 4)
+
+        def terms_of(u):
+            if u in CAST_AFTER_UNIT:
+                return terms_sb[2 + CAST_AFTER_UNIT.index(u) % 2]
+            return terms_sb[u % 2]
+
+        def add_turned(dst, terms):
+            for n, term in enumerate(terms):
+                nc.tensor.matmul(dst, term, ident[:], start=(n == 0), stop=(n == len(terms) - 1), is_transpose=True)
+
+        def product(u):
+            s, j0, j1 = UNITS[u]
+            blk, i = divmod(s, PACK)
+            half, c0, width = j0 // BANK, j0 % BANK, j1 - j0
+            for a in range(2):
+                nc.tensor.matmul_mx(
+                    out=bank["f", u % 2][:, 0:width],
+                    lhsT=w1_codes[a, blk][:, P * i : P * (i + 1)].bitcast(FP8X4),
+                    lhsT_scale=w1_scales[blk][:, a, P * i : P * (i + 1)],
+                    rhs=v_w[a, half][:, c0 : c0 + width].bitcast(FP8X4),
+                    rhs_scale=v_sc[half][4 * a : P, c0 : c0 + width],
+                    start=(a == 0),
+                    stop=(a == 1),
+                )
+
+        def turns(u):
+            s, j0, j1 = UNITS[u]
+            blk, i = divmod(s, PACK)
+            width = j1 - j0
+            t, whole = turns_sb[u % 2], whole_sb[u % 2]
+            nc.scalar.activation(
+                t[:, 0:width],
+                bank["f", u % 2][:, 0:width],
+                ACT.Identity,
+                bias=phase_turns[:, blk, i : i + 1],
+                scale=1.0 / TWO_PI,
+            )
+            nc.scalar.activation(whole[:, 0:width], t[:, 0:width], ACT.Copy, bias=TURNS_MID_BITS, scale=-BITS_PER_TURN)
+            for c0 in range(0, width, P):
+                add_turned(bank["full", u % 2][:, c0 : c0 + P], [t[:, c0 : c0 + P]])
+            for c0 in range(0, width, P):
+                cols = slice(c0, c0 + P)
+                add_turned(bank["frac", u % 2][:, cols], [whole[:, cols].bitcast(F32), minus_mid[:], t[:, cols]])
+
+        def sine(u):
+            width = UNITS[u][2] - UNITS[u][1]
+            angle, sin = terms_of(u)[:, 0:BANK], terms_of(u)[:, BANK : 2 * BANK]
+            nc.scalar.activation(angle[:, 0:width], bank["full", u % 2][:, 0:width], ACT.Copy, scale=TWO_PI)
+            nc.scalar.activation(sin[:, 0:width], bank["frac", u % 2][:, 0:width], ACT.Sin, scale=TWO_PI)
+            for c0 in range(0, width, P):
+                cols = slice(c0, c0 + P)
+                add_turned(bank["both", u % 2][:, cols], [angle[:, cols], sin[:, cols]])
+
+        def feature(u):
+            s, j0, j1 = UNITS[u]
+            blk, i = divmod(s, PACK)
+            nc.scalar.activation(
+                h_ring[s % 4][:, j0:j1],
+                bank["both", u % 2][:, 0 : j1 - j0],
+                ACT.Identity,
+                bias=h_bias[:, blk, i : i + 1],
+                scale=gain_sb[:, blk, i : i + 1],
+            )
+
+        def scatter(s, j0, j1):
+            nc.vector.tensor_tensor(
+                pages[s % PACK][:].indirect(put[:, j0 // 16 : j1 // 16]), h_ring[s % 4][:, j0:j1], wgs_sb[:, j0:j1], ALU.mult
+            )
+
+        def gather(dst, s, m0, m1):
+            nc.vector.tensor_tensor(
+                dst, pages[s % PACK][:].indirect(take[:, m0 // 16 : m1 // 16]), wgt_sb[:, m0:m1], ALU.mult
+            )
+
+        z_sb = pair_of("z", [P, PACK * CHUNK], BF16)
+        zq = {}
+
+        def quantise_z(z, blk, m0, m1):
+            codes = held("z_codes%d_%d" % (blk, m0), [P, m1 - m0], U32)
+            scales = held("z_scales%d_%d" % (blk, m0), [P, m1 - m0], U8)
+            nc.vector.quantize_mx(out=codes[:].bitcast(FP8X4), scales=scales[:], in_=z)
+            for c0, c1 in CHUNKS:
+                if m0 <= c0 and c1 <= m1:
+                    zq[blk, c0] = (codes[:, c0 - m0 : c1 - m0], scales[:, c0 - m0 : c1 - m0])
+
+        zt_sb = pair_of("zt", [P, PACK * P], BF16)
+
+        def press_sum_low(n):
+            m0 = CHUNK * n
+            back = bank["both", n % 2][:].rearrange("p (k u m) -> p k u m", k=2, u=2)
+            for k in range(2):
+                turned = bank[("full", "frac")[k], n % 2][:].rearrange("m (i p) -> m i p", i=PACK)
+                for i in range(PACK):
+                    c0 = M * i + m0 + P * k
+                    add_turned(turned[:, i, :], [press_sb[:, c0 : c0 + P], x_low[:, c0 : c0 + P]])
+                nc.scalar.copy(
+                    out=zt_sb[k][:].rearrange("m (u p e) -> m u p e", u=2, e=2),
+                    in_=turned.rearrange("m (u e) p -> m u p e", e=2),
+                )
+                pairs = zt_sb[k][:].bitcast(F32)
+                for u in range(2):
+                    add_turned(back[:, k, u, :], [pairs[:, P * u : P * (u + 1)]])
+            z = z_sb[n % 2][:]
+            nc.scalar.copy(
+                out=z.bitcast(F32).rearrange("p (k m u) -> p k m u", k=2, u=2), in_=back.rearrange("p k u m -> p k m u")
+            )
+            quantise_z(z, 0, m0, m0 + CHUNK)
+
+        w4 = w1_codes[0, 0][:].bitcast(U8)
+        w4_sc = w1_scales[0]
+        w2_raw = []
+
+        def after_unit(u):
+            s, j0, j1 = UNITS[u]
+            if u in CAST_AFTER_UNIT:
+                n = CAST_AFTER_UNIT.index(u)
+                if n < 2:
+                    quantise_w1(w1_high[n], n, 1, nc.scalar.copy, terms_of(u)[:])
+                else:
+                    quantise_w2(w2_raw[n - 2], n - 2, terms_of(u)[:])
+                if n in (0, 2):
+                    w2_raw.append(load_rows(stage[:], w2, n // 2, 0))
+            if j1 == S and s < PACK:
+                gather(x_low[:, M * s : M * (s + 1)], s, 0, M)
+            if j1 == S and s == PACK - 1:
+                nc.sync.dma_start(
+                    out=w1_codes[0, 0][:].bitcast(I32).rearrange("p (a c) -> p a c", a=2),
+                    in_=w4_words.rearrange("a p c -> p a c").bitcast(I32),
+                )
+                for q in range(4):
+                    nc.sync.dma_start(
+                        out=w4_sc[32 * q : 32 * q + 4, :, :].bitcast(I32),
+                        in_=w4_scales[:, 4 * q : 4 * q + 4, :].rearrange("a r n -> r a n").bitcast(I32),
+                    )
+
+        def units(u0, u1):
+            product(u0)
+            product(u0 + 1)
+            turns(u0)
+            for u in range(u0, u1 + 1):
+                if u > u0:
+                    feature(u - 1)
+                    s, j0, j1 = UNITS[u - 1]
+                    if s == 0:
+                        scatter(s, j0, j1)
+                    elif j1 == S:
+                        scatter(s, 0, S)
+                if u < u1:
+                    sine(u)
+                if u + 1 < u1:
+                    turns(u + 1)
+                if u > u0:
+                    after_unit(u - 1)
+                if u + 2 < u1:
+                    product(u + 2)
+
+        units(0, len(UNITS) - 2)
+        for n in range(M // CHUNK):
+            press_sum_low(n)
+        load_press(1)
+        units(len(UNITS) - 2, len(UNITS))
+
+        x_high = pair_of("x_high", [P, PACK * CHUNK], F32)
+
+        def scores(n):
+            m0, m1 = CHUNKS[n]
+            width = m1 - m0
+            for pair in range(2):
+                y1 = bank[("f", "frac")[pair], n % 2]
+                y2 = bank[("full", "both")[pair], n % 2]
+                for e in range(2):
+                    cols = slice(P * (2 * pair + e), P * (2 * pair + e + 1))
+                    for blk in range(2):
+                        codes, scales = zq[blk, m0]
+                        nc.tensor.matmul_mx(
+                            out=y1[:, width * e : width * (e + 1)],
+                            lhsT=w2_codes[blk][:, cols].bitcast(FP8X4),
+                            lhsT_scale=w2_scales[blk][:, cols],
+                            rhs=codes.bitcast(FP8X4),
+                            rhs_scale=scales,
+                            start=(blk == 0),
+                            stop=(blk == 1),
+                        )
+                for e in range(2):
+                    t = 2 * pair + e
+                    for c0 in range(0, width, P):
+                        for blk in range(2):
+                            codes, scales = zq[blk, m0]
+                            w0 = 2 * (N * blk + P * t)
+                            nc.tensor.matmul_mx(
+                                out=y2[:, width * e + c0 : width * e + c0 + P],
+                                lhsT=w4[:, w0 : w0 + 2 * P].bitcast(FP4X4),
+                                lhsT_scale=w4_sc[:, blk, P * t : P * (t + 1)],
+                                rhs=codes[:, c0 : c0 + P].bitcast(FP8X4),
+                                rhs_scale=scales[:, c0 : c0 + P],
+                                start=(blk == 0),
+                                stop=(blk == 1),
+                            )
+                biased = x_high[n % 2][:, 2 * width * pair : 2 * width * (pair + 1)]
+                for e in range(2):
+                    t = 2 * pair + e
+                    cols = slice(width * e, width * (e + 1))
+                    nc.scalar.activation(biased[:, cols], y1[:, cols], ACT.Identity, bias=b_sb[:, t : t + 1])
+                best = ring.tile([P, 2 * width], F32, name="best")
+                nc.vector.tensor_tensor(best[:], biased, y2[:, 0 : 2 * width], ALU.max)
+                nc.sync.dma_start(
+                    out=out[2 * P * pair : 2 * P * (pair + 1), m0:m1].rearrange("(e p) m -> p e m", p=P),
+                    in_=best[:].rearrange("p (e m) -> p e m", e=2),
+                )
+
+        for n, (m0, m1) in enumerate(CHUNKS):
+            width = m1 - m0
+            x = x_high[n % 2]
+            for i in range(PACK):
+                gather(x[:, width * i : width * (i + 1)], PACK + i, m0, m1)
+            z = z_sb[n % 2][:, 0 : PACK * width]
+            nc.vector.tensor_tensor(
+                z.rearrange("p (c q i) -> p c i q", q=4, i=PACK),
+                x[:, 0 : PACK * width].rearrange("p (i c q) -> p c i q", q=4, i=PACK),
+                press_rows[:, :, m0:m1].rearrange("p i (c q) -> p c i q", q=4),
+                ALU.add,
+            )
+            quantise_z(z, 1, m0, m1)
+            if n > 0:
+                scores(n - 1)
+        scores(len(CHUNKS) - 1)

@@ -50,8 +50,8 @@ def tile_list_fountain_cue_scorer_kernel(
             return [held("%s%d" % (name, n), shape, dtype) for n in range(count)]
 
         bank = {}
-        for role in ("f", "full", "frac", "both"):
-            for n in range(2):
+        for role, count in (("f", 2), ("frac", 2), ("back", 4)):
+            for n in range(count):
                 bank[role, n] = psum.tile([P, BANK], F32, name="bank_%s%d" % (role, n))
 
         tab_sc = held("tab_sc", [P, T], U8)
@@ -80,9 +80,6 @@ def tile_list_fountain_cue_scorer_kernel(
         nc.sync.dma_start(put[:], offs2)
         take = keep.tile([P, M // 16], U16, name="take")
         nc.sync.dma_start(take[:], offs3)
-        b_sb = held("b_sb", [P, N // P], F32)
-        with nc.allow_non_contiguous_dma(reason="one bias value for each output row"):
-            nc.gpsimd.dma_start(out=b_sb[:], in_=b.rearrange("(t p) -> p t", p=P))
 
         weights = held("weights", [P, 2 * S], F32)
         press_sb = held("press_sb", [P, PACK * M], F32)
@@ -125,8 +122,6 @@ def tile_list_fountain_cue_scorer_kernel(
 
         phase_turns = held("phase_turns", [P, 2, PACK], F32)
         nc.vector.tensor_scalar(phase_turns[:], phase_sb[:], 1.0 / TWO_PI, None, ALU.mult)
-        h_bias = held("h_bias", [P, 2, PACK], F32)
-        nc.vector.scalar_tensor_tensor(h_bias[:], phase_sb[:], -1.0, gain_sb[:], ALU.mult, ALU.mult)
 
         quantise_w1(w1_low[0], 0, 0, nc.vector.tensor_copy, stage[:, 0:S])
         quantise_w1(w1_low[1], 1, 0, nc.scalar.copy, x_late[:, 0:S])
@@ -154,13 +149,14 @@ def tile_list_fountain_cue_scorer_kernel(
 
         turns_sb = pair_of("turns", [P, BANK], F32)
         whole_sb = pair_of("whole", [P, BANK], U32)
-        terms_sb = pair_of("terms", [P, 2 * BANK], F32, 4)
+        sin_sb = pair_of("sin", [P, BANK], F32)
+        cast_sb = pair_of("cast", [P, 2 * BANK], F32)
         h_ring = pair_of("h", [P, S], F32, 4)
 
-        def terms_of(u):
+        def sin_of(u):
             if u in CAST_AFTER_UNIT:
-                return terms_sb[2 + CAST_AFTER_UNIT.index(u) % 2]
-            return terms_sb[u % 2]
+                return cast_sb[CAST_AFTER_UNIT.index(u) % 2]
+            return sin_sb[u % 2]
 
         def add_turned(dst, terms):
             for n, term in enumerate(terms):
@@ -194,30 +190,26 @@ def tile_list_fountain_cue_scorer_kernel(
                 scale=1.0 / TWO_PI,
             )
             nc.scalar.activation(whole[:, 0:width], t[:, 0:width], ACT.Copy, bias=TURNS_MID_BITS, scale=-BITS_PER_TURN)
-            for c0 in range(0, width, P):
-                add_turned(bank["full", u % 2][:, c0 : c0 + P], [t[:, c0 : c0 + P]])
+            nc.scalar.activation(
+                h_ring[s % 4][:, j0:j1], bank["f", u % 2][:, 0:width], ACT.Identity, scale=gain_sb[:, blk, i : i + 1]
+            )
             for c0 in range(0, width, P):
                 cols = slice(c0, c0 + P)
                 add_turned(bank["frac", u % 2][:, cols], [whole[:, cols].bitcast(F32), minus_mid[:], t[:, cols]])
 
         def sine(u):
             width = UNITS[u][2] - UNITS[u][1]
-            angle, sin = terms_of(u)[:, 0:BANK], terms_of(u)[:, BANK : 2 * BANK]
-            nc.scalar.activation(angle[:, 0:width], bank["full", u % 2][:, 0:width], ACT.Copy, scale=TWO_PI)
+            sin = sin_of(u)
             nc.scalar.activation(sin[:, 0:width], bank["frac", u % 2][:, 0:width], ACT.Sin, scale=TWO_PI)
             for c0 in range(0, width, P):
-                cols = slice(c0, c0 + P)
-                add_turned(bank["both", u % 2][:, cols], [angle[:, cols], sin[:, cols]])
+                add_turned(bank["back", u % 4][:, c0 : c0 + P], [sin[:, c0 : c0 + P]])
 
         def feature(u):
             s, j0, j1 = UNITS[u]
             blk, i = divmod(s, PACK)
-            nc.scalar.activation(
-                h_ring[s % 4][:, j0:j1],
-                bank["both", u % 2][:, 0 : j1 - j0],
-                ACT.Identity,
-                bias=h_bias[:, blk, i : i + 1],
-                scale=gain_sb[:, blk, i : i + 1],
+            h = h_ring[s % 4][:, j0:j1]
+            nc.vector.scalar_tensor_tensor(
+                h, bank["back", u % 4][:, 0 : j1 - j0], gain_sb[:, blk, i : i + 1], h, ALU.mult, ALU.add
             )
 
         def scatter(s, j0, j1):
@@ -230,7 +222,7 @@ def tile_list_fountain_cue_scorer_kernel(
                 dst, pages[s % PACK][:].indirect(take[:, m0 // 16 : m1 // 16]), wgt_sb[:, m0:m1], ALU.mult
             )
 
-        z_sb = pair_of("z", [P, PACK * CHUNK], BF16)
+        z_sb = pair_of("z", [P, PACK * CHUNK], BF16, M // CHUNK)
         zq = {}
 
         def quantise_z(z, blk, m0, m1):
@@ -245,9 +237,9 @@ def tile_list_fountain_cue_scorer_kernel(
 
         def press_sum_low(n):
             m0 = CHUNK * n
-            back = bank["both", n % 2][:].rearrange("p (k u m) -> p k u m", k=2, u=2)
+            back = bank["f", n % 2][:].rearrange("p (k u m) -> p k u m", k=2, u=2)
             for k in range(2):
-                turned = bank[("full", "frac")[k], n % 2][:].rearrange("m (i p) -> m i p", i=PACK)
+                turned = bank["frac", k][:].rearrange("m (i p) -> m i p", i=PACK)
                 for i in range(PACK):
                     c0 = M * i + m0 + P * k
                     add_turned(turned[:, i, :], [press_sb[:, c0 : c0 + P], x_low[:, c0 : c0 + P]])
@@ -258,7 +250,7 @@ def tile_list_fountain_cue_scorer_kernel(
                 pairs = zt_sb[k][:].bitcast(F32)
                 for u in range(2):
                     add_turned(back[:, k, u, :], [pairs[:, P * u : P * (u + 1)]])
-            z = z_sb[n % 2][:]
+            z = z_sb[n][:]
             nc.scalar.copy(
                 out=z.bitcast(F32).rearrange("p (k m u) -> p k m u", k=2, u=2), in_=back.rearrange("p k u m -> p k m u")
             )
@@ -273,9 +265,9 @@ def tile_list_fountain_cue_scorer_kernel(
             if u in CAST_AFTER_UNIT:
                 n = CAST_AFTER_UNIT.index(u)
                 if n < 2:
-                    quantise_w1(w1_high[n], n, 1, nc.scalar.copy, terms_of(u)[:])
+                    quantise_w1(w1_high[n], n, 1, nc.scalar.copy, sin_of(u)[:])
                 else:
-                    quantise_w2(w2_raw[n - 2], n - 2, terms_of(u)[:])
+                    quantise_w2(w2_raw[n - 2], n - 2, sin_of(u)[:])
                 if n in (0, 2):
                     w2_raw.append(load_rows(stage[:], w2, n // 2, 0))
             if j1 == S and s < PACK:
@@ -320,40 +312,49 @@ def tile_list_fountain_cue_scorer_kernel(
 
         x_high = pair_of("x_high", [P, PACK * CHUNK], F32)
 
+        b_sb = turns_sb[0][:, 0 : N // P]
+        with nc.allow_non_contiguous_dma(reason="one bias value for each output row"):
+            nc.sync.dma_start(out=b_sb, in_=b.rearrange("(t p) -> p t", p=P))
+        score_banks = ([bank["f", 0], bank["f", 1], bank["frac", 0], bank["frac", 1]], [bank["back", n] for n in range(4)])
+
+        def score_passes(n, blk):
+            m0, m1 = CHUNKS[n]
+            width = m1 - m0
+            codes, scales = zq[blk, m0]
+            for pair in range(2):
+                y1, y2 = score_banks[n % 2][2 * pair : 2 * pair + 2]
+                for e in range(2):
+                    cols = slice(P * (2 * pair + e), P * (2 * pair + e + 1))
+                    nc.tensor.matmul_mx(
+                        out=y1[:, width * e : width * (e + 1)],
+                        lhsT=w2_codes[blk][:, cols].bitcast(FP8X4),
+                        lhsT_scale=w2_scales[blk][:, cols],
+                        rhs=codes.bitcast(FP8X4),
+                        rhs_scale=scales,
+                        start=(blk == 0 and e == 0),
+                        stop=(blk == 1 and e == 1),
+                    )
+                for e in range(2):
+                    t = 2 * pair + e
+                    w0 = 2 * (N * blk + P * t)
+                    for c0 in range(0, width, P):
+                        nc.tensor.matmul_mx(
+                            out=y2[:, width * e + c0 : width * e + c0 + P],
+                            lhsT=w4[:, w0 : w0 + 2 * P].bitcast(FP4X4),
+                            lhsT_scale=w4_sc[:, blk, P * t : P * (t + 1)],
+                            rhs=codes[:, c0 : c0 + P].bitcast(FP8X4),
+                            rhs_scale=scales[:, c0 : c0 + P],
+                            start=(blk == 0 and e == 0 and c0 == 0),
+                            stop=(blk == 1 and e == 1 and c0 + P == width),
+                        )
+
         def scores(n):
             m0, m1 = CHUNKS[n]
             width = m1 - m0
+            score_passes(n, 0)
+            score_passes(n, 1)
             for pair in range(2):
-                y1 = bank[("f", "frac")[pair], n % 2]
-                y2 = bank[("full", "both")[pair], n % 2]
-                for e in range(2):
-                    cols = slice(P * (2 * pair + e), P * (2 * pair + e + 1))
-                    for blk in range(2):
-                        codes, scales = zq[blk, m0]
-                        nc.tensor.matmul_mx(
-                            out=y1[:, width * e : width * (e + 1)],
-                            lhsT=w2_codes[blk][:, cols].bitcast(FP8X4),
-                            lhsT_scale=w2_scales[blk][:, cols],
-                            rhs=codes.bitcast(FP8X4),
-                            rhs_scale=scales,
-                            start=(blk == 0),
-                            stop=(blk == 1),
-                        )
-                for e in range(2):
-                    t = 2 * pair + e
-                    for c0 in range(0, width, P):
-                        for blk in range(2):
-                            codes, scales = zq[blk, m0]
-                            w0 = 2 * (N * blk + P * t)
-                            nc.tensor.matmul_mx(
-                                out=y2[:, width * e + c0 : width * e + c0 + P],
-                                lhsT=w4[:, w0 : w0 + 2 * P].bitcast(FP4X4),
-                                lhsT_scale=w4_sc[:, blk, P * t : P * (t + 1)],
-                                rhs=codes[:, c0 : c0 + P].bitcast(FP8X4),
-                                rhs_scale=scales[:, c0 : c0 + P],
-                                start=(blk == 0),
-                                stop=(blk == 1),
-                            )
+                y1, y2 = score_banks[n % 2][2 * pair : 2 * pair + 2]
                 biased = x_high[n % 2][:, 2 * width * pair : 2 * width * (pair + 1)]
                 for e in range(2):
                     t = 2 * pair + e

@@ -23,11 +23,12 @@ PACK = 4
 PASS = P * PACK
 BANK = 512
 SLICES = H // P
-FIRST_PIECES = ((0, 256), (256, 512), (512, 1024))
+FIRST_PIECES = ((0, 256), (256, 512), (512, 768), (768, 1024))
 UNITS = [(0, j0, j1) for j0, j1 in FIRST_PIECES] + [(s, j0, j0 + BANK) for s in range(1, SLICES) for j0 in (0, BANK)]
 CHUNK = 256
-CHUNKS = ((0, 256), (256, 512), (512, 768), (768, 896), (896, 1024))
-CAST_AFTER_UNIT = (4, 6, 10, 12)
+VECTOR_SLICES = (0,)
+CHUNKS = ((0, 256), (256, 512), (512, 768), (768, 1024))
+CAST_AFTER_UNIT = (4, 5, 10, 12)
 TWO_PI = 2.0 * math.pi
 TURNS_MID = 98304.0
 TURNS_MID_BITS = float(0x47C00000)
@@ -99,19 +100,28 @@ def tile_list_fountain_cue_scorer_kernel(
         w2_codes = pair_of("w2_codes", [P, N], U32)
         w2_scales = pair_of("w2_scales", [P, N], U8)
 
+        def in_pieces(copy, dst, src, pieces):
+            step = P // pieces
+            for c0 in range(0, P, step):
+                copy(out=dst[:, c0 : c0 + step], in_=src[:, c0 : c0 + step])
+
         def quantise_w1(raw, a, blk, copy, room):
             grouped = room.bitcast(BF16)
-            copy(
-                out=grouped.rearrange("p (i m j) -> p m j i", i=PACK, j=PACK),
-                in_=raw.rearrange("p j (m i) -> p m j i", i=PACK),
+            in_pieces(
+                copy,
+                grouped.rearrange("p (i m j) -> p m j i", i=PACK, j=PACK),
+                raw.rearrange("p j (m i) -> p m j i", i=PACK),
+                1 + 3 * blk,
             )
             nc.vector.quantize_mx(out=w1_codes[a, blk][:].bitcast(FP8X4), scales=w1_scales[blk][:, a, :], in_=grouped)
 
         def quantise_w2(raw, blk, room):
             grouped = room.bitcast(BF16)
-            nc.scalar.copy(
-                out=grouped.rearrange("p (c q j) -> p c j q", q=4, j=PACK),
-                in_=raw.rearrange("p j (c q) -> p c j q", q=4),
+            in_pieces(
+                nc.scalar.copy,
+                grouped.rearrange("p (c q j) -> p c j q", q=4, j=PACK),
+                raw.rearrange("p j (c q) -> p c j q", q=4),
+                4,
             )
             nc.vector.quantize_mx(out=w2_codes[blk][:].bitcast(FP8X4), scales=w2_scales[blk][:], in_=grouped)
 
@@ -158,6 +168,12 @@ def tile_list_fountain_cue_scorer_kernel(
                 return cast_sb[CAST_AFTER_UNIT.index(u) % 2]
             return sin_sb[u % 2]
 
+        def f_bank(u):
+            return bank[("f", "frac")[u // 2 % 2], u % 2]
+
+        def frac_bank(u):
+            return bank[("frac", "f")[u // 2 % 2], u % 2]
+
         def add_turned(dst, terms):
             for n, term in enumerate(terms):
                 nc.tensor.matmul(dst, term, ident[:], start=(n == 0), stop=(n == len(terms) - 1), is_transpose=True)
@@ -168,7 +184,7 @@ def tile_list_fountain_cue_scorer_kernel(
             half, c0, width = j0 // BANK, j0 % BANK, j1 - j0
             for a in range(2):
                 nc.tensor.matmul_mx(
-                    out=bank["f", u % 2][:, 0:width],
+                    out=f_bank(u)[:, 0:width],
                     lhsT=w1_codes[a, blk][:, P * i : P * (i + 1)].bitcast(FP8X4),
                     lhsT_scale=w1_scales[blk][:, a, P * i : P * (i + 1)],
                     rhs=v_w[a, half][:, c0 : c0 + width].bitcast(FP8X4),
@@ -184,23 +200,31 @@ def tile_list_fountain_cue_scorer_kernel(
             t, whole = turns_sb[u % 2], whole_sb[u % 2]
             nc.scalar.activation(
                 t[:, 0:width],
-                bank["f", u % 2][:, 0:width],
+                f_bank(u)[:, 0:width],
                 ACT.Identity,
                 bias=phase_turns[:, blk, i : i + 1],
                 scale=1.0 / TWO_PI,
             )
             nc.scalar.activation(whole[:, 0:width], t[:, 0:width], ACT.Copy, bias=TURNS_MID_BITS, scale=-BITS_PER_TURN)
             nc.scalar.activation(
-                h_ring[s % 4][:, j0:j1], bank["f", u % 2][:, 0:width], ACT.Identity, scale=gain_sb[:, blk, i : i + 1]
+                h_ring[s % 4][:, j0:j1], f_bank(u)[:, 0:width], ACT.Identity, scale=gain_sb[:, blk, i : i + 1]
             )
+            if s in VECTOR_SLICES:
+                nc.vector.scalar_tensor_tensor(
+                    t[:, 0:width], whole[:, 0:width].bitcast(F32), -TURNS_MID, t[:, 0:width], ALU.add, ALU.add
+                )
+                return
             for c0 in range(0, width, P):
                 cols = slice(c0, c0 + P)
-                add_turned(bank["frac", u % 2][:, cols], [whole[:, cols].bitcast(F32), minus_mid[:], t[:, cols]])
+                add_turned(frac_bank(u)[:, cols], [whole[:, cols].bitcast(F32), minus_mid[:], t[:, cols]])
 
         def sine(u):
             width = UNITS[u][2] - UNITS[u][1]
             sin = sin_of(u)
-            nc.scalar.activation(sin[:, 0:width], bank["frac", u % 2][:, 0:width], ACT.Sin, scale=TWO_PI)
+            if UNITS[u][0] in VECTOR_SLICES:
+                nc.scalar.activation(sin[:, 0:width], turns_sb[u % 2][:, 0:width], ACT.Sin, scale=TWO_PI)
+                return
+            nc.scalar.activation(sin[:, 0:width], frac_bank(u)[:, 0:width], ACT.Sin, scale=TWO_PI)
             for c0 in range(0, width, P):
                 add_turned(bank["back", u % 4][:, c0 : c0 + P], [sin[:, c0 : c0 + P]])
 
@@ -208,8 +232,9 @@ def tile_list_fountain_cue_scorer_kernel(
             s, j0, j1 = UNITS[u]
             blk, i = divmod(s, PACK)
             h = h_ring[s % 4][:, j0:j1]
+            sin = sin_of(u) if s in VECTOR_SLICES else bank["back", u % 4]
             nc.vector.scalar_tensor_tensor(
-                h, bank["back", u % 4][:, 0 : j1 - j0], gain_sb[:, blk, i : i + 1], h, ALU.mult, ALU.add
+                h, sin[:, 0 : j1 - j0], gain_sb[:, blk, i : i + 1], h, ALU.mult, ALU.add
             )
 
         def scatter(s, j0, j1):
@@ -256,8 +281,8 @@ def tile_list_fountain_cue_scorer_kernel(
             )
             quantise_z(z, 0, m0, m0 + CHUNK)
 
-        w4 = w1_codes[0, 0][:].bitcast(U8)
-        w4_sc = w1_scales[0]
+        w4 = w1_codes[0, 1][:].bitcast(U8)
+        w4_sc = w1_scales[1]
         w2_raw = []
 
         def after_unit(u):
@@ -272,9 +297,9 @@ def tile_list_fountain_cue_scorer_kernel(
                     w2_raw.append(load_rows(stage[:], w2, n // 2, 0))
             if j1 == S and s < PACK:
                 gather(x_low[:, M * s : M * (s + 1)], s, 0, M)
-            if j1 == S and s == PACK - 1:
+            if j1 == S and s == SLICES - 1:
                 nc.sync.dma_start(
-                    out=w1_codes[0, 0][:].bitcast(I32).rearrange("p (a c) -> p a c", a=2),
+                    out=w1_codes[0, 1][:].bitcast(I32).rearrange("p (a c) -> p a c", a=2),
                     in_=w4_words.rearrange("a p c -> p a c").bitcast(I32),
                 )
                 for q in range(4):
@@ -288,6 +313,10 @@ def tile_list_fountain_cue_scorer_kernel(
             product(u0 + 1)
             turns(u0)
             for u in range(u0, u1 + 1):
+                if u + 1 < u1:
+                    turns(u + 1)
+                if u < u1:
+                    sine(u)
                 if u > u0:
                     feature(u - 1)
                     s, j0, j1 = UNITS[u - 1]
@@ -295,11 +324,6 @@ def tile_list_fountain_cue_scorer_kernel(
                         scatter(s, j0, j1)
                     elif j1 == S:
                         scatter(s, 0, S)
-                if u < u1:
-                    sine(u)
-                if u + 1 < u1:
-                    turns(u + 1)
-                if u > u0:
                     after_unit(u - 1)
                 if u + 2 < u1:
                     product(u + 2)
@@ -310,12 +334,12 @@ def tile_list_fountain_cue_scorer_kernel(
         load_press(1)
         units(len(UNITS) - 2, len(UNITS))
 
-        x_high = pair_of("x_high", [P, PACK * CHUNK], F32)
+        x_high = pair_of("x_high", [P, PACK * CHUNK], F32, 3)
 
         b_sb = turns_sb[0][:, 0 : N // P]
         with nc.allow_non_contiguous_dma(reason="one bias value for each output row"):
             nc.sync.dma_start(out=b_sb, in_=b.rearrange("(t p) -> p t", p=P))
-        score_banks = ([bank["f", 0], bank["f", 1], bank["frac", 0], bank["frac", 1]], [bank["back", n] for n in range(4)])
+        score_banks = ([bank["f", 0], bank["f", 1], bank["frac", 0], bank["frac", 1]], [bank["back", (len(UNITS) + n) % 4] for n in (2, 0, 3, 1)])
 
         def score_passes(n, blk):
             m0, m1 = CHUNKS[n]
@@ -355,7 +379,7 @@ def tile_list_fountain_cue_scorer_kernel(
             score_passes(n, 1)
             for pair in range(2):
                 y1, y2 = score_banks[n % 2][2 * pair : 2 * pair + 2]
-                biased = x_high[n % 2][:, 2 * width * pair : 2 * width * (pair + 1)]
+                biased = x_high[n % 3][:, 2 * width * pair : 2 * width * (pair + 1)]
                 for e in range(2):
                     t = 2 * pair + e
                     cols = slice(width * e, width * (e + 1))
@@ -369,10 +393,10 @@ def tile_list_fountain_cue_scorer_kernel(
 
         for n, (m0, m1) in enumerate(CHUNKS):
             width = m1 - m0
-            x = x_high[n % 2]
+            x = x_high[n % 3]
             for i in range(PACK):
                 gather(x[:, width * i : width * (i + 1)], PACK + i, m0, m1)
-            z = z_sb[n % 2][:, 0 : PACK * width]
+            z = z_sb[n % 3][:, 0 : PACK * width]
             nc.vector.tensor_tensor(
                 z.rearrange("p (c q i) -> p c i q", q=4, i=PACK),
                 x[:, 0 : PACK * width].rearrange("p (i c q) -> p c i q", q=4, i=PACK),

@@ -26,9 +26,10 @@ SLICES = H // P
 FIRST_PIECES = ((0, 256), (256, 512), (512, 768), (768, 1024))
 UNITS = [(0, j0, j1) for j0, j1 in FIRST_PIECES] + [(s, j0, j0 + BANK) for s in range(1, SLICES) for j0 in (0, BANK)]
 CHUNK = 256
+GPSIMD_FROM = 2
 VECTOR_SLICES = (0,)
 CHUNKS = ((0, 256), (256, 512), (512, 768), (768, 1024))
-CAST_AFTER_UNIT = (4, 5, 10, 12)
+CAST_AFTER_UNIT = (3, 4, 10, 12)
 TWO_PI = 2.0 * math.pi
 TURNS_MID = 98304.0
 TURNS_MID_BITS = float(0x47C00000)
@@ -84,9 +85,10 @@ def tile_list_fountain_cue_scorer_kernel(
 
         weights = held("weights", [P, 2 * S], F32)
         press_sb = held("press_sb", [P, PACK * M], F32)
-        stage = held("stage", [P, PACK * BANK], F32)
+        press_high = held("press_high", [P, PACK * M], F32)
+        stage = press_high[:, 0 : PACK * BANK]
         x_low = held("x_low", [P, PACK * M], F32)
-        x_late = x_low[:, 2 * M : 4 * M]
+        x_late = press_high[:, PACK * BANK : 2 * PACK * BANK]
 
         def load_rows(room, src, a, c0):
             raw = room.rearrange("p (j c) -> p j c", j=PACK)
@@ -138,12 +140,12 @@ def tile_list_fountain_cue_scorer_kernel(
         wgs_sb, wgt_sb = weights[:, 0:S], weights[:, S : S + M]
         nc.sync.dma_start(out=wgs_sb, in_=wgs)
         nc.sync.dma_start(out=wgt_sb, in_=wgt)
-        w1_high = [load_rows(stage[:], w1, 0, BANK), load_rows(x_late, w1, 1, BANK)]
-        press_rows = press_sb[:].rearrange("p (i m) -> p i m", i=PACK)
+        w1_high = [load_rows(stage, w1, 0, BANK), load_rows(x_late, w1, 1, BANK)]
+        press_rows = press_high[:].rearrange("p (i m) -> p i m", i=PACK)
 
         def load_press(blk):
             nc.sync.dma_start(
-                out=press_rows, in_=press[PASS * blk : PASS * (blk + 1), :].rearrange("(p i) m -> p i m", i=PACK)
+                out=(press_sb, press_high)[blk][:].rearrange("p (i m) -> p i m", i=PACK), in_=press[PASS * blk : PASS * (blk + 1), :].rearrange("(p i) m -> p i m", i=PACK)
             )
 
         load_press(0)
@@ -162,6 +164,9 @@ def tile_list_fountain_cue_scorer_kernel(
         sin_sb = pair_of("sin", [P, BANK], F32)
         cast_sb = pair_of("cast", [P, 2 * BANK], F32)
         h_ring = pair_of("h", [P, S], F32, 4)
+        put_ring = pair_of("weighted", [P, S], F32, 3)
+
+        x_high = pair_of("x_high", [P, PACK * CHUNK], F32, 3)
 
         def sin_of(u):
             if u in CAST_AFTER_UNIT:
@@ -231,16 +236,27 @@ def tile_list_fountain_cue_scorer_kernel(
         def feature(u):
             s, j0, j1 = UNITS[u]
             blk, i = divmod(s, PACK)
-            h = h_ring[s % 4][:, j0:j1]
-            sin = sin_of(u) if s in VECTOR_SLICES else bank["back", u % 4]
-            nc.vector.scalar_tensor_tensor(
-                h, sin[:, 0 : j1 - j0], gain_sb[:, blk, i : i + 1], h, ALU.mult, ALU.add
-            )
+            h, weighted = h_ring[s % 4][:, j0:j1], put_ring[s % 3][:, j0:j1]
+            if s in VECTOR_SLICES:
+                nc.vector.scalar_tensor_tensor(
+                    h, sin_of(u)[:, 0 : j1 - j0], gain_sb[:, blk, i : i + 1], h, ALU.mult, ALU.add
+                )
+            elif s in range(1, GPSIMD_FROM + 1):
+                nc.vector.scalar_tensor_tensor(
+                    h, bank["back", u % 4][:], gain_sb[:, blk, i : i + 1], h, ALU.mult, ALU.add
+                )
+            else:
+                nc.scalar.activation(weighted, bank["back", u % 4][:], ACT.Identity, scale=gain_sb[:, blk, i : i + 1])
+                nc.gpsimd.tensor_tensor(h, h, weighted, ALU.add)
+            if s >= GPSIMD_FROM:
+                nc.gpsimd.tensor_tensor(weighted, h, wgs_sb[:, j0:j1], ALU.mult)
 
         def scatter(s, j0, j1):
-            nc.vector.tensor_tensor(
-                pages[s % PACK][:].indirect(put[:, j0 // 16 : j1 // 16]), h_ring[s % 4][:, j0:j1], wgs_sb[:, j0:j1], ALU.mult
-            )
+            places = pages[s % PACK][:].indirect(put[:, j0 // 16 : j1 // 16])
+            if s >= GPSIMD_FROM:
+                nc.vector.tensor_copy(places, put_ring[s % 3][:, j0:j1])
+            else:
+                nc.vector.tensor_tensor(places, h_ring[s % 4][:, j0:j1], wgs_sb[:, j0:j1], ALU.mult)
 
         def gather(dst, s, m0, m1):
             nc.vector.tensor_tensor(
@@ -260,11 +276,19 @@ def tile_list_fountain_cue_scorer_kernel(
 
         zt_sb = pair_of("zt", [P, PACK * P], BF16)
 
+        score_banks = (
+            [bank["f", 0], bank["f", 1], bank["frac", 0], bank["frac", 1]],
+            [bank["back", (len(UNITS) + n) % 4] for n in (2, 0, 3, 1)],
+        )
+
         def press_sum_low(n):
             m0 = CHUNK * n
-            back = bank["f", n % 2][:].rearrange("p (k u m) -> p k u m", k=2, u=2)
+            z = z_sb[n][:]
+            if n >= 2:
+                z = put_ring[(SLICES - 1) % 3][:, BANK * (n - 2) : BANK * (n - 1)].bitcast(BF16)
             for k in range(2):
-                turned = bank["frac", k][:].rearrange("m (i p) -> m i p", i=PACK)
+                turned = score_banks[n % 2][2 * k][:].rearrange("m (i p) -> m i p", i=PACK)
+                back = score_banks[n % 2][2 * k + 1][:, 0 : 2 * P]
                 for i in range(PACK):
                     c0 = M * i + m0 + P * k
                     add_turned(turned[:, i, :], [press_sb[:, c0 : c0 + P], x_low[:, c0 : c0 + P]])
@@ -274,11 +298,11 @@ def tile_list_fountain_cue_scorer_kernel(
                 )
                 pairs = zt_sb[k][:].bitcast(F32)
                 for u in range(2):
-                    add_turned(back[:, k, u, :], [pairs[:, P * u : P * (u + 1)]])
-            z = z_sb[n][:]
-            nc.scalar.copy(
-                out=z.bitcast(F32).rearrange("p (k m u) -> p k m u", k=2, u=2), in_=back.rearrange("p k u m -> p k m u")
-            )
+                    add_turned(back[:, P * u : P * (u + 1)], [pairs[:, P * u : P * (u + 1)]])
+                nc.scalar.copy(
+                    out=z.bitcast(F32)[:, 2 * P * k : 2 * P * (k + 1)].rearrange("p (m u) -> p m u", u=2),
+                    in_=back.rearrange("p (u m) -> p m u", u=2),
+                )
             quantise_z(z, 0, m0, m0 + CHUNK)
 
         w4 = w1_codes[0, 1][:].bitcast(U8)
@@ -293,8 +317,10 @@ def tile_list_fountain_cue_scorer_kernel(
                     quantise_w1(w1_high[n], n, 1, nc.scalar.copy, sin_of(u)[:])
                 else:
                     quantise_w2(w2_raw[n - 2], n - 2, sin_of(u)[:])
+                if n == 3:
+                    load_press(1)
                 if n in (0, 2):
-                    w2_raw.append(load_rows(stage[:], w2, n // 2, 0))
+                    w2_raw.append(load_rows(stage, w2, n // 2, 0))
             if j1 == S and s < PACK:
                 gather(x_low[:, M * s : M * (s + 1)], s, 0, M)
             if j1 == S and s == SLICES - 1:
@@ -328,18 +354,14 @@ def tile_list_fountain_cue_scorer_kernel(
                 if u + 2 < u1:
                     product(u + 2)
 
-        units(0, len(UNITS) - 2)
+        units(0, len(UNITS))
         for n in range(M // CHUNK):
             press_sum_low(n)
-        load_press(1)
-        units(len(UNITS) - 2, len(UNITS))
 
-        x_high = pair_of("x_high", [P, PACK * CHUNK], F32, 3)
 
         b_sb = turns_sb[0][:, 0 : N // P]
         with nc.allow_non_contiguous_dma(reason="one bias value for each output row"):
             nc.sync.dma_start(out=b_sb, in_=b.rearrange("(t p) -> p t", p=P))
-        score_banks = ([bank["f", 0], bank["f", 1], bank["frac", 0], bank["frac", 1]], [bank["back", (len(UNITS) + n) % 4] for n in (2, 0, 3, 1)])
 
         def score_passes(n, blk):
             m0, m1 = CHUNKS[n]

import math
from contextlib import ExitStack

import concourse.mybir as mybir
from concourse.masks import make_identity

K, T, S, H, T2, M, N = 1024, 2048, 1024, 1024, 2048, 1024, 512
FLOPS = 2 * K * H * S + 2 * 2 * H * N * M

F32 = mybir.dt.float32
BF16 = mybir.dt.bfloat16
I32 = mybir.dt.int32
U32 = mybir.dt.uint32
U16 = mybir.dt.uint16
U8 = mybir.dt.uint8
FP8X4 = mybir.dt.float8_e4m3fn_x4
FP4X4 = mybir.dt.float4_e2m1fn_x4
ACT = mybir.ActivationFunctionType
ALU = mybir.AluOpType

P = 128
PACK = 4
PASS = P * PACK
BANK = 512
SLICES = H // P
FIRST_PIECES = ((0, 256), (256, 512), (512, 768), (768, 1024))
UNITS = [(0, j0, j1) for j0, j1 in FIRST_PIECES] + [(s, j0, j0 + BANK) for s in range(1, SLICES) for j0 in (0, BANK)]
CHUNK = 256
GPSIMD_FROM = 2
VECTOR_SLICES = (0,)
CHUNKS = ((0, 256), (256, 512), (512, 768), (768, 1024))
CAST_AFTER_UNIT = (3, 4, 10, 12)
TWO_PI = 2.0 * math.pi
TURNS_MID = 98304.0
TURNS_MID_BITS = float(0x47C00000)
BITS_PER_TURN = 128.0


def tile_list_fountain_cue_scorer_kernel(
    tc, tab_words, tab_scales, offs, w1, phase, gain, wgs, offs2, wgt, offs3, press, w2, w4_words, w4_scales, b, out
):
    nc = tc.nc
    with ExitStack() as ctx:
        keep = ctx.enter_context(tc.tile_pool(name="keep", bufs=1))
        ring = ctx.enter_context(tc.tile_pool(name="ring", bufs=3))
        psum = ctx.enter_context(tc.psum_pool(name="psum", bufs=1))

        def held(name, shape, dtype):
            return keep.tile(shape, dtype, name=name, align_bytes=64)

        def pair_of(name, shape, dtype, count=2):
            return [held("%s%d" % (name, n), shape, dtype) for n in range(count)]

        bank = {}
        for role, count in (("f", 2), ("frac", 2), ("back", 4)):
            for n in range(count):
                bank[role, n] = psum.tile([P, BANK], F32, name="bank_%s%d" % (role, n))

        tab_sc = held("tab_sc", [P, T], U8)
        nc.gpsimd.memset(tab_sc[:].bitcast(I32), 0)
        minus_mid = held("minus_mid", [P, P], F32)
        nc.vector.memset(minus_mid[:], -TURNS_MID)
        ident = held("ident", [P, P], F32)
        make_identity(nc, ident[:])
        pages = pair_of("page", [P, T2], F32, PACK)
        for page in pages:
            nc.vector.memset(page[:], 0.0)

        for q in range(4):
            nc.scalar.dma_start(
                out=tab_sc[32 * q : 32 * q + 8, :].bitcast(I32), in_=tab_scales[:, 4 * q : 4 * q + 4, :].bitcast(I32)
            )
        warm = held("warm", [P, 1], F32)
        nc.scalar.activation(warm[:], minus_mid[:, 0:1], ACT.Sin, scale=0.0)
        pick = keep.tile([P, S // 16], U16, name="pick")
        nc.sync.dma_start(pick[:], offs)
        phase_sb = held("phase_sb", [P, 2, PACK], F32)
        nc.sync.dma_start(out=phase_sb[:], in_=phase.rearrange("(b p i) -> p b i", b=2, i=PACK))
        gain_sb = held("gain_sb", [P, 2, PACK], F32)
        nc.sync.dma_start(out=gain_sb[:], in_=gain.rearrange("(b p i) -> p b i", b=2, i=PACK))
        put = keep.tile([P, S // 16], U16, name="put")
        nc.sync.dma_start(put[:], offs2)
        take = keep.tile([P, M // 16], U16, name="take")
        nc.sync.dma_start(take[:], offs3)

        weights = held("weights", [P, 2 * S], F32)
        press_sb = held("press_sb", [P, PACK * M], F32)
        press_high = held("press_high", [P, PACK * M], F32)
        stage = press_high[:, 0 : PACK * BANK]
        x_low = held("x_low", [P, PACK * M], F32)
        x_late = press_high[:, PACK * BANK : 2 * PACK * BANK]

        def load_rows(room, src, a, c0):
            raw = room.rearrange("p (j c) -> p j c", j=PACK)
            nc.sync.dma_start(
                out=raw, in_=src[PASS * a : PASS * (a + 1), c0 : c0 + BANK].rearrange("(p j) c -> p j c", j=PACK)
            )
            return raw

        w1_codes = {(a, blk): held("w1_codes%d%d" % (a, blk), [P, BANK], U32) for a in range(2) for blk in range(2)}
        w1_scales = pair_of("w1_scales", [P, 2, BANK], U8)
        w2_codes = pair_of("w2_codes", [P, N], U32)
        w2_scales = pair_of("w2_scales", [P, N], U8)

        def in_pieces(copy, dst, src, pieces):
            step = P // pieces
            for c0 in range(0, P, step):
                copy(out=dst[:, c0 : c0 + step], in_=src[:, c0 : c0 + step])

        def quantise_w1(raw, a, blk, copy, room):
            grouped = room.bitcast(BF16)
            in_pieces(
                copy,
                grouped.rearrange("p (i m j) -> p m j i", i=PACK, j=PACK),
                raw.rearrange("p j (m i) -> p m j i", i=PACK),
                1 + 3 * blk,
            )
            nc.vector.quantize_mx(out=w1_codes[a, blk][:].bitcast(FP8X4), scales=w1_scales[blk][:, a, :], in_=grouped)

        def quantise_w2(raw, blk, room):
            grouped = room.bitcast(BF16)
            in_pieces(
                nc.scalar.copy,
                grouped.rearrange("p (c q j) -> p c j q", q=4, j=PACK),
                raw.rearrange("p j (c q) -> p c j q", q=4),
                4,
            )
            nc.vector.quantize_mx(out=w2_codes[blk][:].bitcast(FP8X4), scales=w2_scales[blk][:], in_=grouped)

        w1_low = [load_rows(weights[:], w1, 0, 0), load_rows(press_sb[:, 0 : PACK * BANK], w1, 1, 0)]
        tab_w = pair_of("tab_w", [P, T], I32)
        for a in range(2):
            nc.sync.dma_start(out=tab_w[a][:], in_=tab_words[a].rearrange("p t i -> p (t i)").bitcast(I32))

        phase_turns = held("phase_turns", [P, 2, PACK], F32)
        nc.vector.tensor_scalar(phase_turns[:], phase_sb[:], 1.0 / TWO_PI, None, ALU.mult)

        quantise_w1(w1_low[0], 0, 0, nc.vector.tensor_copy, stage[:, 0:S])
        quantise_w1(w1_low[1], 1, 0, nc.scalar.copy, x_late[:, 0:S])
        wgs_sb, wgt_sb = weights[:, 0:S], weights[:, S : S + M]
        nc.sync.dma_start(out=wgs_sb, in_=wgs)
        nc.sync.dma_start(out=wgt_sb, in_=wgt)
        w1_high = [load_rows(stage, w1, 0, BANK), load_rows(x_late, w1, 1, BANK)]
        press_rows = press_high[:].rearrange("p (i m) -> p i m", i=PACK)

        def load_press(blk):
            nc.sync.dma_start(
                out=(press_sb, press_high)[blk][:].rearrange("p (i m) -> p i m", i=PACK), in_=press[PASS * blk : PASS * (blk + 1), :].rearrange("(p i) m -> p i m", i=PACK)
            )

        load_press(0)

        v_sc = pair_of("v_sc", [P, BANK], U8)
        v_w = {(a, half): held("v_w%d%d" % (a, half), [P, BANK], U32) for a in range(2) for half in range(2)}
        for j0, j1 in FIRST_PIECES:
            half, c0, c1 = j0 // BANK, j0 % BANK, (j1 - 1) % BANK + 1
            cols = pick[:, j0 // 16 : j1 // 16]
            nc.vector.tensor_copy(v_sc[half][:, c0:c1], tab_sc[:].indirect(cols))
            for a in range(2):
                nc.vector.tensor_copy(v_w[a, half][:, c0:c1], tab_w[a][:].bitcast(U32).indirect(cols))

        turns_sb = pair_of("turns", [P, BANK], F32)
        whole_sb = pair_of("whole", [P, BANK], U32)
        sin_sb = pair_of("sin", [P, BANK], F32)
        cast_sb = pair_of("cast", [P, 2 * BANK], F32)
        h_ring = pair_of("h", [P, S], F32, 4)
        put_ring = pair_of("weighted", [P, S], F32, 3)

        x_high = pair_of("x_high", [P, PACK * CHUNK], F32, 3)

        def sin_of(u):
            if u in CAST_AFTER_UNIT:
                return cast_sb[CAST_AFTER_UNIT.index(u) % 2]
            return sin_sb[u % 2]

        def f_bank(u):
            return bank[("f", "frac")[u // 2 % 2], u % 2]

        def frac_bank(u):
            return bank[("frac", "f")[u // 2 % 2], u % 2]

        def add_turned(dst, terms):
            for n, term in enumerate(terms):
                nc.tensor.matmul(dst, term, ident[:], start=(n == 0), stop=(n == len(terms) - 1), is_transpose=True)

        def product(u):
            s, j0, j1 = UNITS[u]
            blk, i = divmod(s, PACK)
            half, c0, width = j0 // BANK, j0 % BANK, j1 - j0
            for a in range(2):
                nc.tensor.matmul_mx(
                    out=f_bank(u)[:, 0:width],
                    lhsT=w1_codes[a, blk][:, P * i : P * (i + 1)].bitcast(FP8X4),
                    lhsT_scale=w1_scales[blk][:, a, P * i : P * (i + 1)],
                    rhs=v_w[a, half][:, c0 : c0 + width].bitcast(FP8X4),
                    rhs_scale=v_sc[half][4 * a : P, c0 : c0 + width],
                    start=(a == 0),
                    stop=(a == 1),
                )

        def turns(u):
            s, j0, j1 = UNITS[u]
            blk, i = divmod(s, PACK)
            width = j1 - j0
            t, whole = turns_sb[u % 2], whole_sb[u % 2]
            nc.scalar.activation(
                t[:, 0:width],
                f_bank(u)[:, 0:width],
                ACT.Identity,
                bias=phase_turns[:, blk, i : i + 1],
                scale=1.0 / TWO_PI,
            )
            nc.scalar.activation(whole[:, 0:width], t[:, 0:width], ACT.Copy, bias=TURNS_MID_BITS, scale=-BITS_PER_TURN)
            nc.scalar.activation(
                h_ring[s % 4][:, j0:j1], f_bank(u)[:, 0:width], ACT.Identity, scale=gain_sb[:, blk, i : i + 1]
            )
            if s in VECTOR_SLICES:
                nc.vector.scalar_tensor_tensor(
                    t[:, 0:width], whole[:, 0:width].bitcast(F32), -TURNS_MID, t[:, 0:width], ALU.add, ALU.add
                )
                return
            for c0 in range(0, width, P):
                cols = slice(c0, c0 + P)
                add_turned(frac_bank(u)[:, cols], [whole[:, cols].bitcast(F32), minus_mid[:], t[:, cols]])

        def sine(u):
            width = UNITS[u][2] - UNITS[u][1]
            sin = sin_of(u)
            if UNITS[u][0] in VECTOR_SLICES:
                nc.scalar.activation(sin[:, 0:width], turns_sb[u % 2][:, 0:width], ACT.Sin, scale=TWO_PI)
                return
            nc.scalar.activation(sin[:, 0:width], frac_bank(u)[:, 0:width], ACT.Sin, scale=TWO_PI)
            for c0 in range(0, width, P):
                add_turned(bank["back", u % 4][:, c0 : c0 + P], [sin[:, c0 : c0 + P]])

        def feature(u):
            s, j0, j1 = UNITS[u]
            blk, i = divmod(s, PACK)
            h, weighted = h_ring[s % 4][:, j0:j1], put_ring[s % 3][:, j0:j1]
            if s in VECTOR_SLICES:
                nc.vector.scalar_tensor_tensor(
                    h, sin_of(u)[:, 0 : j1 - j0], gain_sb[:, blk, i : i + 1], h, ALU.mult, ALU.add
                )
            elif s in range(1, GPSIMD_FROM + 1):
                nc.vector.scalar_tensor_tensor(
                    h, bank["back", u % 4][:], gain_sb[:, blk, i : i + 1], h, ALU.mult, ALU.add
                )
            else:
                nc.scalar.activation(weighted, bank["back", u % 4][:], ACT.Identity, scale=gain_sb[:, blk, i : i + 1])
                nc.gpsimd.tensor_tensor(h, h, weighted, ALU.add)
            if s >= GPSIMD_FROM:
                nc.gpsimd.tensor_tensor(weighted, h, wgs_sb[:, j0:j1], ALU.mult)

        def scatter(s, j0, j1):
            places = pages[s % PACK][:].indirect(put[:, j0 // 16 : j1 // 16])
            if s >= GPSIMD_FROM:
                nc.vector.tensor_copy(places, put_ring[s % 3][:, j0:j1])
            else:
                nc.vector.tensor_tensor(places, h_ring[s % 4][:, j0:j1], wgs_sb[:, j0:j1], ALU.mult)

        def gather(dst, s, m0, m1):
            nc.vector.tensor_tensor(
                dst, pages[s % PACK][:].indirect(take[:, m0 // 16 : m1 // 16]), wgt_sb[:, m0:m1], ALU.mult
            )

        z_sb = pair_of("z", [P, PACK * CHUNK], BF16, M // CHUNK)
        zq = {}

        def quantise_z(z, blk, m0, m1):
            codes = held("z_codes%d_%d" % (blk, m0), [P, m1 - m0], U32)
            scales = held("z_scales%d_%d" % (blk, m0), [P, m1 - m0], U8)
            nc.vector.quantize_mx(out=codes[:].bitcast(FP8X4), scales=scales[:], in_=z)
            for c0, c1 in CHUNKS:
                if m0 <= c0 and c1 <= m1:
                    zq[blk, c0] = (codes[:, c0 - m0 : c1 - m0], scales[:, c0 - m0 : c1 - m0])

        zt_sb = pair_of("zt", [P, PACK * P], BF16)

        score_banks = (
            [bank["f", 0], bank["f", 1], bank["frac", 0], bank["frac", 1]],
            [bank["back", (len(UNITS) + n) % 4] for n in (2, 0, 3, 1)],
        )

        def press_sum_low(n):
            m0 = CHUNK * n
            z = z_sb[n][:]
            if n >= 2:
                z = put_ring[(SLICES - 1) % 3][:, BANK * (n - 2) : BANK * (n - 1)].bitcast(BF16)
            for k in range(2):
                turned = score_banks[n % 2][2 * k][:].rearrange("m (i p) -> m i p", i=PACK)
                back = score_banks[n % 2][2 * k + 1][:, 0 : 2 * P]
                for i in range(PACK):
                    c0 = M * i + m0 + P * k
                    add_turned(turned[:, i, :], [press_sb[:, c0 : c0 + P], x_low[:, c0 : c0 + P]])
                nc.scalar.copy(
                    out=zt_sb[k][:].rearrange("m (u p e) -> m u p e", u=2, e=2),
                    in_=turned.rearrange("m (u e) p -> m u p e", e=2),
                )
                pairs = zt_sb[k][:].bitcast(F32)
                for u in range(2):
                    add_turned(back[:, P * u : P * (u + 1)], [pairs[:, P * u : P * (u + 1)]])
                nc.scalar.copy(
                    out=z.bitcast(F32)[:, 2 * P * k : 2 * P * (k + 1)].rearrange("p (m u) -> p m u", u=2),
                    in_=back.rearrange("p (u m) -> p m u", u=2),
                )
            quantise_z(z, 0, m0, m0 + CHUNK)

        w4 = w1_codes[0, 1][:].bitcast(U8)
        w4_sc = w1_scales[1]
        w2_raw = []

        def after_unit(u):
            s, j0, j1 = UNITS[u]
            if u in CAST_AFTER_UNIT:
                n = CAST_AFTER_UNIT.index(u)
                if n < 2:
                    quantise_w1(w1_high[n], n, 1, nc.scalar.copy, sin_of(u)[:])
                else:
                    quantise_w2(w2_raw[n - 2], n - 2, sin_of(u)[:])
                if n == 3:
                    load_press(1)
                if n in (0, 2):
                    w2_raw.append(load_rows(stage, w2, n // 2, 0))
            if j1 == S and s < PACK:
                gather(x_low[:, M * s : M * (s + 1)], s, 0, M)
            if j1 == S and s == SLICES - 1:
                nc.sync.dma_start(
                    out=w1_codes[0, 1][:].bitcast(I32).rearrange("p (a c) -> p a c", a=2),
                    in_=w4_words.rearrange("a p c -> p a c").bitcast(I32),
                )
                for q in range(4):
                    nc.sync.dma_start(
                        out=w4_sc[32 * q : 32 * q + 4, :, :].bitcast(I32),
                        in_=w4_scales[:, 4 * q : 4 * q + 4, :].rearrange("a r n -> r a n").bitcast(I32),
                    )

        def units(u0, u1):
            product(u0)
            product(u0 + 1)
            turns(u0)
            for u in range(u0, u1 + 1):
                if u + 1 < u1:
                    turns(u + 1)
                if u < u1:
                    sine(u)
                if u > u0:
                    feature(u - 1)
                    s, j0, j1 = UNITS[u - 1]
                    if s == 0:
                        scatter(s, j0, j1)
                    elif j1 == S:
                        scatter(s, 0, S)
                    after_unit(u - 1)
                if u + 2 < u1:
                    product(u + 2)

        units(0, len(UNITS))
        for n in range(M // CHUNK):
            press_sum_low(n)


        b_sb = turns_sb[0][:, 0 : N // P]
        with nc.allow_non_contiguous_dma(reason="one bias value for each output row"):
            nc.sync.dma_start(out=b_sb, in_=b.rearrange("(t p) -> p t", p=P))

        def score_passes(n, blk):
            m0, m1 = CHUNKS[n]
            width = m1 - m0
            codes, scales = zq[blk, m0]
            for pair in range(2):
                y1, y2 = score_banks[n % 2][2 * pair : 2 * pair + 2]
                for e in range(2):
                    cols = slice(P * (2 * pair + e), P * (2 * pair + e + 1))
                    nc.tensor.matmul_mx(
                        out=y1[:, width * e : width * (e + 1)],
                        lhsT=w2_codes[blk][:, cols].bitcast(FP8X4),
                        lhsT_scale=w2_scales[blk][:, cols],
                        rhs=codes.bitcast(FP8X4),
                        rhs_scale=scales,
                        start=(blk == 0 and e == 0),
                        stop=(blk == 1 and e == 1),
                    )
                for e in range(2):
                    t = 2 * pair + e
                    w0 = 2 * (N * blk + P * t)
                    for c0 in range(0, width, P):
                        nc.tensor.matmul_mx(
                            out=y2[:, width * e + c0 : width * e + c0 + P],
                            lhsT=w4[:, w0 : w0 + 2 * P].bitcast(FP4X4),
                            lhsT_scale=w4_sc[:, blk, P * t : P * (t + 1)],
                            rhs=codes[:, c0 : c0 + P].bitcast(FP8X4),
                            rhs_scale=scales[:, c0 : c0 + P],
                            start=(blk == 0 and e == 0 and c0 == 0),
                            stop=(blk == 1 and e == 1 and c0 + P == width),
                        )

        def scores(n):
            m0, m1 = CHUNKS[n]
            width = m1 - m0
            score_passes(n, 0)
            score_passes(n, 1)
            for pair in range(2):
                y1, y2 = score_banks[n % 2][2 * pair : 2 * pair + 2]
                biased = x_high[n % 3][:, 2 * width * pair : 2 * width * (pair + 1)]
                for e in range(2):
                    t = 2 * pair + e
                    cols = slice(width * e, width * (e + 1))
                    nc.scalar.activation(biased[:, cols], y1[:, cols], ACT.Identity, bias=b_sb[:, t : t + 1])
                best = ring.tile([P, 2 * width], F32, name="best")
                nc.vector.tensor_tensor(best[:], biased, y2[:, 0 : 2 * width], ALU.max)
                nc.sync.dma_start(
                    out=out[2 * P * pair : 2 * P * (pair + 1), m0:m1].rearrange("(e p) m -> p e m", p=P),
                    in_=best[:].rearrange("p (e m) -> p e m", e=2),
                )

        for n, (m0, m1) in enumerate(CHUNKS):
            width = m1 - m0
            x = x_high[n % 3]
            for i in range(PACK):
                gather(x[:, width * i : width * (i + 1)], PACK + i, m0, m1)
            z = z_sb[n % 3][:, 0 : PACK * width]
            nc.vector.tensor_tensor(
                z.rearrange("p (c q i) -> p c i q", q=4, i=PACK),
                x[:, 0 : PACK * width].rearrange("p (i c q) -> p c i q", q=4, i=PACK),
                press_rows[:, :, m0:m1].rearrange("p i (c q) -> p c i q", q=4),
                ALU.add,
            )
            quantise_z(z, 1, m0, m1)
            if n > 0:
                scores(n - 1)
        scores(len(CHUNKS) - 1)
